import numpy as np
import ml_dtypes


def mxq(x, axis, fmt="e4m3"):
    dtype, down = {"e4m3": (ml_dtypes.float8_e4m3fn, 7), "e5m2": (ml_dtypes.float8_e5m2, 14)}[fmt]
    v = np.moveaxis(np.asarray(x, np.float32).astype(ml_dtypes.bfloat16).astype(np.float64), axis, -1)
    blocks = v.reshape(v.shape[:-1] + (-1, 32))
    amax = np.abs(blocks).max(-1, keepdims=True)
    byte = np.maximum(np.where(amax > 0, np.frexp(amax)[1] - 1 + 127, 0) - down, 1)
    scale = np.exp2(byte - 127.0)
    codes = (blocks / scale).astype(np.float32).astype(dtype).astype(np.float64)
    return np.moveaxis((codes * scale).reshape(v.shape), -1, axis)


WIDE = False


def mx_kscale(k):
    if not WIDE:
        return np.ones(k)
    levels = np.array([10, -10, 5, -5, 0])
    if k % 512:
        return np.exp2(np.random.permutation(np.resize(levels, k // 32))).repeat(32)
    a = np.empty((k // 512, 16))
    for p in range(k // 512):
        a[p, :8] = np.random.permutation(np.resize(levels, 8))
        for g in range(8):
            far = levels[np.abs(levels - a[p, g]) >= 10]
            a[p, g + 8] = far[np.random.randint(len(far))]
    return np.exp2(a.ravel()).repeat(32)


def f64(x):
    return np.asarray(x).astype(np.float64)


def striped8(idx):
    return np.concatenate([v.reshape(-1, 16).T for v in idx]).astype(np.uint16)


def unstriped8(offs):
    return np.stack([offs[16 * g:16 * g + 16].T.reshape(-1) for g in range(8)]).astype(np.int64)


E2M1 = np.array([0.0, 0.5, 1.0, 1.5, 2.0, 3.0, 4.0, 6.0, -0.0, -0.5, -1.0, -1.5, -2.0, -3.0, -4.0, -6.0])


def pack_weight(w, fmt):
    k, n = w.shape
    w = f64(np.asarray(w, np.float32).astype(ml_dtypes.bfloat16)).reshape(k // 32, 32, n)
    amax = np.abs(w).max(1)
    if fmt == "e4m3":
        byte = np.frexp(amax)[1] - 1 + 127 - 7
    else:
        mant, ex = np.frexp(amax / 6.0)
        byte = np.where(mant > 0.5, ex, ex - 1) + 127
    byte = np.clip(np.where(amax > 0, byte, 1), 1, 254)
    scaled = (w * np.exp2(127.0 - byte)[:, None, :]).reshape(k, n).astype(np.float32)
    by_word = np.ascontiguousarray(scaled.reshape(k // 512, 128, 4, n).transpose(0, 1, 3, 2))
    if fmt == "e4m3":
        words = by_word.astype(ml_dtypes.float8_e4m3fn).view(np.uint8)
    else:
        c = by_word.astype(ml_dtypes.float4_e2m1fn).view(np.uint8) & 0xF
        words = (c[..., 0::2] | (c[..., 1::2] << 4)).reshape(k // 512, 128, 2 * n)
    return np.ascontiguousarray(words), np.ascontiguousarray(byte.astype(np.uint8).reshape(k // 512, 16, n))


def unpack_weight(words, scales, fmt):
    g, _, n = scales.shape
    words = np.ascontiguousarray(words).reshape(g, 128, n, -1)
    if fmt == "e4m3":
        vals = words.view(ml_dtypes.float8_e4m3fn).astype(np.float64)
    else:
        nib = np.empty((g, 128, n, 4), np.uint8)
        nib[..., 0::2] = words & 0xF
        nib[..., 1::2] = words >> 4
        vals = E2M1[nib]
    vals = vals * np.repeat(np.exp2(scales.astype(np.float64) - 127.0), 8, axis=1)[..., None]
    return vals.transpose(0, 1, 3, 2).reshape(g * 512, n)


def silu(v):
    return v / (1.0 + np.exp(-np.maximum(v, -700.0)))


K, M, T, S = 512, 128, 2048, 1024


def setup_inputs():
    n = np.random.standard_normal
    s = mx_kscale(K)[:, None]
    p_w4 = pack_weight(n((K, M)) / np.sqrt(K) / s, "e2m1")
    return {
        "x": (n((K, S)) * s).astype(np.float32),
        "w4_words": p_w4[0],
        "w4_scales": p_w4[1],
        "w8": (n((K, M)) / np.sqrt(K) / s).astype(np.float32),
        "wgo": np.repeat(np.random.uniform(0.5, 2.0, (8, S)), 16, axis=0).astype(np.float32),
        "offs": striped8(np.stack([np.random.permutation(T)[:S] for _ in range(8)])),
    }


def reference(x, w4_words, w4_scales, w8, wgo, offs):
    x_ = mxq(f64(x), 0, "e4m3")
    w4_ = unpack_weight(w4_words, w4_scales, "e2m1")
    w8_ = mxq(f64(w8), 0, "e4m3")
    y = w4_.T @ x_
    u = w8_.T @ x_
    y = silu(y) * u
    place = unstriped8(offs)[np.arange(M) % 128 // 16]
    out = np.zeros((M, T))
    out[np.arange(M)[:, None], place] = f64(wgo)[np.arange(M) % 128] * (y)
    return out

@@ -1,0 +1,169 @@
+from contextlib import ExitStack
+
+import concourse.mybir as mybir
+
+K, M, T, S = 512, 128, 2048, 1024
+FLOPS = 2 * 2 * K * M * S
+
+F32 = mybir.dt.float32
+BF16 = mybir.dt.bfloat16
+I32 = mybir.dt.int32
+U32 = mybir.dt.uint32
+U16 = mybir.dt.uint16
+U8 = mybir.dt.uint8
+FP8X4 = mybir.dt.float8_e4m3fn_x4
+FP4X4 = mybir.dt.float4_e2m1fn_x4
+MULT = mybir.AluOpType.mult
+SILU = mybir.ActivationFunctionType.Silu
+
+P = 128
+PACK = 4
+LIST_ROWS = 16
+X_LOADS = [128,128,128,128,256,256]
+WGO_LOADS = [512,512]
+CHUNKS = [128,128,128,128,256,256]
+
+
+def starts(widths):
+    return [sum(widths[:i]) for i in range(len(widths))]
+
+
+def piece(tiles, widths, j0):
+    for tile, a, w in zip(tiles, starts(widths), widths):
+        if a <= j0 < a + w:
+            return tile, j0 - a
+    raise ValueError(j0)
+
+
+def tile_list_hscat_g_none_kernel(tc, x, w4_words, w4_scales, w8, wgo, offs, out):
+    nc = tc.nc
+    with ExitStack() as ctx:
+        keep = ctx.enter_context(tc.tile_pool(name="keep", bufs=1))
+        psum = ctx.enter_context(tc.psum_pool(name="psum", bufs=4))
+
+        offsets = keep.tile([P, S // LIST_ROWS], U16, name="offsets")
+        w4_codes = keep.tile([P, 2 * M], U8, name="w4_codes", align_bytes=64)
+        w4_plane = keep.tile([P, M], U8, name="w4_plane", align_bytes=64)
+        w8_raw = keep.tile([P, PACK, M], F32, name="w8_raw")
+        x_raw = [keep.tile([P, PACK, w], F32, name="x_raw%d" % i) for i, w in enumerate(X_LOADS)]
+        wgo_sb = [keep.tile([P, w], F32, name="wgo%d" % i) for i, w in enumerate(WGO_LOADS)]
+        window = keep.tile([P, T], F32, name="window")
+
+        def load_x(i):
+            a = starts(X_LOADS)[i]
+            nc.sync.dma_start(out=x_raw[i][:], in_=x.rearrange("(p t) j -> p t j", t=PACK)[:, :, a : a + X_LOADS[i]])
+
+        def load_wgo(i):
+            a = starts(WGO_LOADS)[i]
+            nc.sync.dma_start(out=wgo_sb[i][:], in_=wgo[:, a : a + WGO_LOADS[i]])
+
+        def load_scales(q, engine):
+            rows = w4_scales[0, 4 * q : 4 * q + 4, :].bitcast(I32)
+            engine.dma_start(out=w4_plane[32 * q : 32 * q + 32, :].bitcast(I32), in_=rows.partition_broadcast(8))
+
+        def load_w8(engine):
+            engine.dma_start(out=w8_raw[:], in_=w8.rearrange("(p t) n -> p t n", t=PACK))
+
+        def load_w4(engine):
+            engine.dma_start(out=w4_codes[:].bitcast(I32), in_=w4_words[0].bitcast(I32))
+
+        load_scales(0, nc.sync)
+        load_scales(1, nc.scalar)
+        load_x(0)
+        load_scales(2, nc.scalar)
+        load_w4(nc.sync)
+        load_scales(3, nc.scalar)
+        load_w8(nc.sync)
+        load_x(1)
+        load_wgo(0)
+        nc.sync.dma_start(offsets[:], offs)
+        load_x(2)
+        load_x(3)
+        load_x(4)
+        load_wgo(1)
+        load_x(5)
+
+        warm_in = keep.tile([P, 2], F32, name="warm_in")
+        warm_out = keep.tile([P, 2], F32, name="warm_out")
+        nc.vector.memset(warm_in[:], 0.0)
+        nc.scalar.activation(out=warm_out[:], in_=warm_in[:], func=SILU)
+        nc.vector.memset(window[:], 0.0)
+
+        def interleave(copy, raw, name):
+            width = raw.shape[2]
+            grouped = keep.tile([P, width, PACK], BF16, name=name, align_bytes=64)
+            copy(
+                out=grouped[:].rearrange("p (c i) t -> p c t i", i=4),
+                in_=raw.rearrange("p t (c i) -> p c t i", i=4),
+            )
+            return grouped
+
+        def quantize(grouped, name):
+            width = grouped.shape[1]
+            codes = keep.tile([P, width], U32, name=name + "_codes", align_bytes=64)
+            plane = keep.tile([P, width], U8, name=name + "_plane", align_bytes=64)
+            nc.vector.quantize_mx(
+                out=codes[:].bitcast(FP8X4), scales=plane[:], in_=grouped[:].rearrange("p j t -> p (j t)")
+            )
+            return codes, plane
+
+        def on_vector(out, in_):
+            nc.vector.tensor_copy(out=out, in_=in_)
+
+        def on_scalar(out, in_):
+            nc.scalar.copy(out=out, in_=in_)
+
+        firsts = starts(CHUNKS)
+        grouped = {}
+        quantized = {}
+        sums = {}
+        factors = {}
+
+        def cast(i):
+            tile, a = piece(x_raw, X_LOADS, firsts[i])
+            grouped[i] = interleave(on_vector if i == 0 else on_scalar, tile[:, :, a : a + CHUNKS[i]], "x_bf%d" % i)
+
+        def multiply(i):
+            codes, plane = quantized[i] if i in quantized else quantize(grouped[i], "x%d" % i)
+            e = psum.tile([M, CHUNKS[i]], F32, name="e")
+            u = psum.tile([M, CHUNKS[i]], F32, name="u")
+            nc.tensor.matmul_mx(
+                out=e[:], lhsT=w4_codes[:].bitcast(FP4X4), lhsT_scale=w4_plane[:],
+                rhs=codes[:].bitcast(FP8X4), rhs_scale=plane[:], start=True, stop=True,
+            )
+            nc.tensor.matmul_mx(
+                out=u[:], lhsT=w8_codes[:].bitcast(FP8X4), lhsT_scale=w8_plane[:],
+                rhs=codes[:].bitcast(FP8X4), rhs_scale=plane[:], start=True, stop=True,
+            )
+            sums[i] = (e, u)
+
+        def place(i):
+            e, u = sums[i]
+            n = CHUNKS[i]
+            if i + 1 < len(CHUNKS):
+                tile, a = piece(x_raw, X_LOADS, firsts[i + 1])
+                gate = tile[:, 0, a : a + n]
+            else:
+                last = keep.tile([M, n], F32, name="gate_last")
+                gate = last[:]
+            up = keep.tile([M, n], F32, name="up%d" % i)
+            nc.scalar.activation(out=gate, in_=e[:], func=SILU)
+            tile, a = piece(wgo_sb, WGO_LOADS, firsts[i])
+            nc.vector.tensor_tensor(up[:], u[:], tile[:, a : a + n], MULT)
+            cols = slice(firsts[i] // LIST_ROWS, (firsts[i] + n) // LIST_ROWS)
+            nc.vector.tensor_tensor(window[:].indirect(offsets[:, cols]), gate, up[:], MULT)
+
+        cast(0)
+        quantized[0] = quantize(grouped[0], "x0")
+        w8_bf = interleave(on_vector, w8_raw[:], "w8_bf")
+        w8_codes, w8_plane = quantize(w8_bf, "w8")
+        multiply(0)
+        cast(1)
+        for i in range(len(CHUNKS)):
+            if i + 1 < len(CHUNKS):
+                multiply(i + 1)
+            place(i)
+            if i + 2 < len(CHUNKS):
+                cast(i + 2)
+
+        nc.sync.dma_start(out=out, in_=window[:])

@@ -20,7 +20,7 @@ P = 128
 PACK = 4
 LIST_ROWS = 16
 X_LOADS = [128,128,128,128,256,256]
-WGO_LOADS = [512,512]
+WGO_LOADS = [256,256,512]
 CHUNKS = [128,128,128,128,256,256]
 
 
@@ -39,7 +39,7 @@ def tile_list_hscat_g_none_kernel(tc, x, w4_words, w4_scales, w8, wgo, offs, out
     nc = tc.nc
     with ExitStack() as ctx:
         keep = ctx.enter_context(tc.tile_pool(name="keep", bufs=1))
-        psum = ctx.enter_context(tc.psum_pool(name="psum", bufs=4))
+        psum = ctx.enter_context(tc.psum_pool(name="psum", bufs=1))
 
         offsets = keep.tile([P, S // LIST_ROWS], U16, name="offsets")
         w4_codes = keep.tile([P, 2 * M], U8, name="w4_codes", align_bytes=64)
@@ -53,9 +53,9 @@ def tile_list_hscat_g_none_kernel(tc, x, w4_words, w4_scales, w8, wgo, offs, out
             a = starts(X_LOADS)[i]
             nc.sync.dma_start(out=x_raw[i][:], in_=x.rearrange("(p t) j -> p t j", t=PACK)[:, :, a : a + X_LOADS[i]])
 
-        def load_wgo(i):
+        def load_wgo(i, engine=nc.sync):
             a = starts(WGO_LOADS)[i]
-            nc.sync.dma_start(out=wgo_sb[i][:], in_=wgo[:, a : a + WGO_LOADS[i]])
+            engine.dma_start(out=wgo_sb[i][:], in_=wgo[:, a : a + WGO_LOADS[i]])
 
         def load_scales(q, engine):
             rows = w4_scales[0, 4 * q : 4 * q + 4, :].bitcast(I32)
@@ -71,16 +71,17 @@ def tile_list_hscat_g_none_kernel(tc, x, w4_words, w4_scales, w8, wgo, offs, out
         load_scales(1, nc.scalar)
         load_x(0)
         load_scales(2, nc.scalar)
-        load_w4(nc.sync)
-        load_scales(3, nc.scalar)
         load_w8(nc.sync)
+        load_scales(3, nc.scalar)
         load_x(1)
+        load_w4(nc.scalar)
         load_wgo(0)
         nc.sync.dma_start(offsets[:], offs)
         load_x(2)
+        load_wgo(1)
         load_x(3)
         load_x(4)
-        load_wgo(1)
+        load_wgo(2)
         load_x(5)
 
         warm_in = keep.tile([P, 2], F32, name="warm_in")
@@ -123,22 +124,22 @@ def tile_list_hscat_g_none_kernel(tc, x, w4_words, w4_scales, w8, wgo, offs, out
             tile, a = piece(x_raw, X_LOADS, firsts[i])
             grouped[i] = interleave(on_vector if i == 0 else on_scalar, tile[:, :, a : a + CHUNKS[i]], "x_bf%d" % i)
 
-        def multiply(i):
-            codes, plane = quantized[i] if i in quantized else quantize(grouped[i], "x%d" % i)
-            e = psum.tile([M, CHUNKS[i]], F32, name="e")
-            u = psum.tile([M, CHUNKS[i]], F32, name="u")
+        def product(name, bank, i, w_codes, w_plane):
+            codes, plane = quantized[i]
+            acc = psum.tile([M, CHUNKS[i]], F32, name="%s%d" % (name, i), tag="bank%d" % (bank % 8))
             nc.tensor.matmul_mx(
-                out=e[:], lhsT=w4_codes[:].bitcast(FP4X4), lhsT_scale=w4_plane[:],
+                out=acc[:], lhsT=w_codes, lhsT_scale=w_plane[:],
                 rhs=codes[:].bitcast(FP8X4), rhs_scale=plane[:], start=True, stop=True,
             )
-            nc.tensor.matmul_mx(
-                out=u[:], lhsT=w8_codes[:].bitcast(FP8X4), lhsT_scale=w8_plane[:],
-                rhs=codes[:].bitcast(FP8X4), rhs_scale=plane[:], start=True, stop=True,
-            )
-            sums[i] = (e, u)
+            sums[name, i] = acc
+
+        def gate_sum(i):
+            product("e", i + 1, i, w4_codes[:].bitcast(FP4X4), w4_plane)
+
+        def up_sum(i):
+            product("u", i, i, w8_codes[:].bitcast(FP8X4), w8_plane)
 
         def place(i):
-            e, u = sums[i]
             n = CHUNKS[i]
             if i + 1 < len(CHUNKS):
                 tile, a = piece(x_raw, X_LOADS, firsts[i + 1])
@@ -147,22 +148,26 @@ def tile_list_hscat_g_none_kernel(tc, x, w4_words, w4_scales, w8, wgo, offs, out
                 last = keep.tile([M, n], F32, name="gate_last")
                 gate = last[:]
             up = keep.tile([M, n], F32, name="up%d" % i)
-            nc.scalar.activation(out=gate, in_=e[:], func=SILU)
+            nc.scalar.activation(out=gate, in_=sums["e", i][:], func=SILU)
             tile, a = piece(wgo_sb, WGO_LOADS, firsts[i])
-            nc.vector.tensor_tensor(up[:], u[:], tile[:, a : a + n], MULT)
+            nc.vector.tensor_tensor(up[:], sums["u", i][:], tile[:, a : a + n], MULT)
             cols = slice(firsts[i] // LIST_ROWS, (firsts[i] + n) // LIST_ROWS)
             nc.vector.tensor_tensor(window[:].indirect(offsets[:, cols]), gate, up[:], MULT)
 
         cast(0)
         quantized[0] = quantize(grouped[0], "x0")
+        gate_sum(0)
         w8_bf = interleave(on_vector, w8_raw[:], "w8_bf")
         w8_codes, w8_plane = quantize(w8_bf, "w8")
-        multiply(0)
+        up_sum(0)
         cast(1)
         for i in range(len(CHUNKS)):
             if i + 1 < len(CHUNKS):
-                multiply(i + 1)
+                quantized[i + 1] = quantize(grouped[i + 1], "x%d" % (i + 1))
+                gate_sum(i + 1)
             place(i)
+            if i + 1 < len(CHUNKS):
+                up_sum(i + 1)
             if i + 2 < len(CHUNKS):
                 cast(i + 2)
 

@@ -18,25 +18,27 @@ SILU = mybir.ActivationFunctionType.Silu
 
 P = 128
 PACK = 4
+QUADRANT = 32
+SCALE_ROWS = 4
 LIST_ROWS = 16
-X_LOADS = [128,128,128,128,256,256]
-WGO_LOADS = [256,256,512]
-CHUNKS = [128,128,128,128,256,256]
+RUN = 4
+
+CHUNKS = [128, 128, 256, 256, 256]
+VECTOR_CHUNKS = 2
+X_LOAD = 256
+WGO_LOADS = [128, 128, 256, 512]
 
 
 def starts(widths):
     return [sum(widths[:i]) for i in range(len(widths))]
 
 
-def piece(tiles, widths, j0):
-    for tile, a, w in zip(tiles, starts(widths), widths):
-        if a <= j0 < a + w:
-            return tile, j0 - a
-    raise ValueError(j0)
-
-
 def tile_list_hscat_g_none_kernel(tc, x, w4_words, w4_scales, w8, wgo, offs, out):
     nc = tc.nc
+    first_token = starts(CHUNKS)
+    wgo_first = starts(WGO_LOADS)
+    last = len(CHUNKS) - 1
+
     with ExitStack() as ctx:
         keep = ctx.enter_context(tc.tile_pool(name="keep", bufs=1))
         psum = ctx.enter_context(tc.psum_pool(name="psum", bufs=1))
@@ -45,57 +47,44 @@ def tile_list_hscat_g_none_kernel(tc, x, w4_words, w4_scales, w8, wgo, offs, out
         w4_codes = keep.tile([P, 2 * M], U8, name="w4_codes", align_bytes=64)
         w4_plane = keep.tile([P, M], U8, name="w4_plane", align_bytes=64)
         w8_raw = keep.tile([P, PACK, M], F32, name="w8_raw")
-        x_raw = [keep.tile([P, PACK, w], F32, name="x_raw%d" % i) for i, w in enumerate(X_LOADS)]
-        wgo_sb = [keep.tile([P, w], F32, name="wgo%d" % i) for i, w in enumerate(WGO_LOADS)]
+        x_raw = [keep.tile([P, PACK, X_LOAD], F32, name="x_raw%d" % a) for a in range(S // X_LOAD)]
+        wgo_sb = [keep.tile([P, w], F32, name="wgo%d" % a) for a, w in enumerate(WGO_LOADS)]
         window = keep.tile([P, T], F32, name="window")
 
-        def load_x(i):
-            a = starts(X_LOADS)[i]
-            nc.sync.dma_start(out=x_raw[i][:], in_=x.rearrange("(p t) j -> p t j", t=PACK)[:, :, a : a + X_LOADS[i]])
-
-        def load_wgo(i, engine=nc.sync):
-            a = starts(WGO_LOADS)[i]
-            engine.dma_start(out=wgo_sb[i][:], in_=wgo[:, a : a + WGO_LOADS[i]])
-
         def load_scales(q, engine):
-            rows = w4_scales[0, 4 * q : 4 * q + 4, :].bitcast(I32)
-            engine.dma_start(out=w4_plane[32 * q : 32 * q + 32, :].bitcast(I32), in_=rows.partition_broadcast(8))
+            rows = w4_scales[0, SCALE_ROWS * q : SCALE_ROWS * (q + 1), :].bitcast(I32)
+            engine.dma_start(
+                out=w4_plane[QUADRANT * q : QUADRANT * (q + 1), :].bitcast(I32),
+                in_=rows.partition_broadcast(QUADRANT // SCALE_ROWS),
+            )
 
-        def load_w8(engine):
-            engine.dma_start(out=w8_raw[:], in_=w8.rearrange("(p t) n -> p t n", t=PACK))
+        def load_x(a):
+            rows = x.rearrange("(p t) j -> p t j", t=PACK)
+            nc.sync.dma_start(out=x_raw[a][:], in_=rows[:, :, a * X_LOAD : (a + 1) * X_LOAD])
 
-        def load_w4(engine):
-            engine.dma_start(out=w4_codes[:].bitcast(I32), in_=w4_words[0].bitcast(I32))
+        def load_wgo(a):
+            nc.sync.dma_start(out=wgo_sb[a][:], in_=wgo[:, wgo_first[a] : wgo_first[a] + WGO_LOADS[a]])
 
         load_scales(0, nc.sync)
         load_scales(1, nc.scalar)
-        load_x(0)
+        nc.sync.dma_start(out=w8_raw[:], in_=w8.rearrange("(p t) n -> p t n", t=PACK))
         load_scales(2, nc.scalar)
-        load_w8(nc.sync)
+        load_x(0)
         load_scales(3, nc.scalar)
-        load_x(1)
-        load_w4(nc.scalar)
-        load_wgo(0)
         nc.sync.dma_start(offsets[:], offs)
-        load_x(2)
-        load_wgo(1)
-        load_x(3)
-        load_x(4)
-        load_wgo(2)
-        load_x(5)
+        nc.scalar.dma_start(out=w4_codes[:].bitcast(I32), in_=w4_words[0].bitcast(I32))
+        load_wgo(0)
+        for a in range(1, len(x_raw)):
+            load_x(a)
+            load_wgo(a)
 
-        warm_in = keep.tile([P, 2], F32, name="warm_in")
-        warm_out = keep.tile([P, 2], F32, name="warm_out")
-        nc.vector.memset(warm_in[:], 0.0)
-        nc.scalar.activation(out=warm_out[:], in_=warm_in[:], func=SILU)
         nc.vector.memset(window[:], 0.0)
 
-        def interleave(copy, raw, name):
-            width = raw.shape[2]
-            grouped = keep.tile([P, width, PACK], BF16, name=name, align_bytes=64)
+        def interleave(copy, raw, name, tag):
+            grouped = keep.tile([P, raw.shape[2], PACK], BF16, name=name, tag=tag, align_bytes=64)
             copy(
-                out=grouped[:].rearrange("p (c i) t -> p c t i", i=4),
-                in_=raw.rearrange("p t (c i) -> p c t i", i=4),
+                out=grouped[:].rearrange("p (c i) t -> p c t i", i=RUN),
+                in_=raw.rearrange("p t (c i) -> p c t i", i=RUN),
             )
             return grouped
 
@@ -108,67 +97,59 @@ def tile_list_hscat_g_none_kernel(tc, x, w4_words, w4_scales, w8, wgo, offs, out
             )
             return codes, plane
 
-        def on_vector(out, in_):
-            nc.vector.tensor_copy(out=out, in_=in_)
+        def raw_tokens(i):
+            a, j0 = divmod(first_token[i], X_LOAD)
+            return x_raw[a][:, :, j0 : j0 + CHUNKS[i]]
 
-        def on_scalar(out, in_):
-            nc.scalar.copy(out=out, in_=in_)
+        def round_chunk(i):
+            if i < VECTOR_CHUNKS:
+                return interleave(nc.vector.tensor_copy, raw_tokens(i), "x_bf%d" % i, "x_bf_vector")
+            return interleave(nc.scalar.copy, raw_tokens(i), "x_bf%d" % i, "x_bf%d" % i)
 
-        firsts = starts(CHUNKS)
-        grouped = {}
-        quantized = {}
-        sums = {}
-        factors = {}
-
-        def cast(i):
-            tile, a = piece(x_raw, X_LOADS, firsts[i])
-            grouped[i] = interleave(on_vector if i == 0 else on_scalar, tile[:, :, a : a + CHUNKS[i]], "x_bf%d" % i)
-
-        def product(name, bank, i, w_codes, w_plane):
-            codes, plane = quantized[i]
-            acc = psum.tile([M, CHUNKS[i]], F32, name="%s%d" % (name, i), tag="bank%d" % (bank % 8))
+        def product(name, bank, w_codes, w_plane, x_mx):
+            codes, plane = x_mx
+            acc = psum.tile([M, codes.shape[1]], F32, name=name, tag="bank%d" % bank)
             nc.tensor.matmul_mx(
                 out=acc[:], lhsT=w_codes, lhsT_scale=w_plane[:],
                 rhs=codes[:].bitcast(FP8X4), rhs_scale=plane[:], start=True, stop=True,
             )
-            sums[name, i] = acc
+            return acc
 
-        def gate_sum(i):
-            product("e", i + 1, i, w4_codes[:].bitcast(FP4X4), w4_plane)
+        def gate_sum(i, x_mx):
+            return product("e%d" % i, i + 1, w4_codes[:].bitcast(FP4X4), w4_plane, x_mx)
 
-        def up_sum(i):
-            product("u", i, i, w8_codes[:].bitcast(FP8X4), w8_plane)
+        def up_sum(i, x_mx):
+            return product("u%d" % i, i, w8_codes[:].bitcast(FP8X4), w8_plane, x_mx)
 
-        def place(i):
+        def place(i, e, u):
             n = CHUNKS[i]
-            if i + 1 < len(CHUNKS):
-                tile, a = piece(x_raw, X_LOADS, firsts[i + 1])
-                gate = tile[:, 0, a : a + n]
+            if VECTOR_CHUNKS <= i + 1 <= last:
+                gate = raw_tokens(i + 1)[:, 0, 0:n]
             else:
-                last = keep.tile([M, n], F32, name="gate_last")
-                gate = last[:]
-            up = keep.tile([M, n], F32, name="up%d" % i)
-            nc.scalar.activation(out=gate, in_=sums["e", i][:], func=SILU)
-            tile, a = piece(wgo_sb, WGO_LOADS, firsts[i])
-            nc.vector.tensor_tensor(up[:], sums["u", i][:], tile[:, a : a + n], MULT)
-            cols = slice(firsts[i] // LIST_ROWS, (firsts[i] + n) // LIST_ROWS)
-            nc.vector.tensor_tensor(window[:].indirect(offsets[:, cols]), gate, up[:], MULT)
+                gate_tile = keep.tile([M, n], F32, name="gate%d" % i)
+                gate = gate_tile[:]
+            nc.scalar.activation(out=gate, in_=e[:], func=SILU)
 
-        cast(0)
-        quantized[0] = quantize(grouped[0], "x0")
-        gate_sum(0)
-        w8_bf = interleave(on_vector, w8_raw[:], "w8_bf")
-        w8_codes, w8_plane = quantize(w8_bf, "w8")
-        up_sum(0)
-        cast(1)
-        for i in range(len(CHUNKS)):
-            if i + 1 < len(CHUNKS):
-                quantized[i + 1] = quantize(grouped[i + 1], "x%d" % (i + 1))
-                gate_sum(i + 1)
-            place(i)
-            if i + 1 < len(CHUNKS):
-                up_sum(i + 1)
-            if i + 2 < len(CHUNKS):
-                cast(i + 2)
+            a = max(b for b, j in enumerate(wgo_first) if j <= first_token[i])
+            j0 = first_token[i] - wgo_first[a]
+            up = keep.tile([M, n], F32, name="up%d" % i)
+            nc.vector.tensor_tensor(up[:], u[:], wgo_sb[a][:, j0 : j0 + n], MULT)
+
+            entries = slice(first_token[i] // LIST_ROWS, (first_token[i] + n) // LIST_ROWS)
+            nc.vector.tensor_tensor(window[:].indirect(offsets[:, entries]), gate, up[:], MULT)
+
+        w8_codes, w8_plane = quantize(interleave(nc.vector.tensor_copy, w8_raw[:], "w8_bf", "w8_bf"), "w8")
+        x_mx = quantize(round_chunk(0), "x0")
+        e = gate_sum(0, x_mx)
+        u = up_sum(0, x_mx)
+        grouped_next = round_chunk(1)
+        for i in range(last):
+            x_mx = quantize(grouped_next, "x%d" % (i + 1))
+            e_next = gate_sum(i + 1, x_mx)
+            place(i, e, u)
+            e, u = e_next, up_sum(i + 1, x_mx)
+            if i + 2 <= last:
+                grouped_next = round_chunk(i + 2)
+        place(last, e, u)
 
         nc.sync.dma_start(out=out, in_=window[:])

from contextlib import ExitStack

import concourse.mybir as mybir

K, M, T, S = 512, 128, 2048, 1024
FLOPS = 2 * 2 * K * M * S

F32 = mybir.dt.float32
BF16 = mybir.dt.bfloat16
I32 = mybir.dt.int32
U32 = mybir.dt.uint32
U16 = mybir.dt.uint16
U8 = mybir.dt.uint8
FP8X4 = mybir.dt.float8_e4m3fn_x4
FP4X4 = mybir.dt.float4_e2m1fn_x4
MULT = mybir.AluOpType.mult
SILU = mybir.ActivationFunctionType.Silu

P = 128
PACK = 4
QUADRANT = 32
SCALE_ROWS = 4
LIST_ROWS = 16
RUN = 4

CHUNKS = [128, 128, 256, 256, 256]
VECTOR_CHUNKS = 2
X_LOAD = 256
WGO_LOADS = [128, 128, 256, 512]


def starts(widths):
    return [sum(widths[:i]) for i in range(len(widths))]


def tile_list_hscat_g_none_kernel(tc, x, w4_words, w4_scales, w8, wgo, offs, out):
    nc = tc.nc
    first_token = starts(CHUNKS)
    wgo_first = starts(WGO_LOADS)
    last = len(CHUNKS) - 1

    with ExitStack() as ctx:
        keep = ctx.enter_context(tc.tile_pool(name="keep", bufs=1))
        psum = ctx.enter_context(tc.psum_pool(name="psum", bufs=1))

        offsets = keep.tile([P, S // LIST_ROWS], U16, name="offsets")
        w4_codes = keep.tile([P, 2 * M], U8, name="w4_codes", align_bytes=64)
        w4_plane = keep.tile([P, M], U8, name="w4_plane", align_bytes=64)
        w8_raw = keep.tile([P, PACK, M], F32, name="w8_raw")
        x_raw = [keep.tile([P, PACK, X_LOAD], F32, name="x_raw%d" % a) for a in range(S // X_LOAD)]
        wgo_sb = [keep.tile([P, w], F32, name="wgo%d" % a) for a, w in enumerate(WGO_LOADS)]
        window = keep.tile([P, T], F32, name="window")

        def load_scales(q, engine):
            rows = w4_scales[0, SCALE_ROWS * q : SCALE_ROWS * (q + 1), :].bitcast(I32)
            engine.dma_start(
                out=w4_plane[QUADRANT * q : QUADRANT * (q + 1), :].bitcast(I32),
                in_=rows.partition_broadcast(QUADRANT // SCALE_ROWS),
            )

        def load_x(a):
            rows = x.rearrange("(p t) j -> p t j", t=PACK)
            nc.sync.dma_start(out=x_raw[a][:], in_=rows[:, :, a * X_LOAD : (a + 1) * X_LOAD])

        def load_wgo(a):
            nc.sync.dma_start(out=wgo_sb[a][:], in_=wgo[:, wgo_first[a] : wgo_first[a] + WGO_LOADS[a]])

        load_scales(0, nc.sync)
        load_scales(1, nc.scalar)
        nc.sync.dma_start(out=w8_raw[:], in_=w8.rearrange("(p t) n -> p t n", t=PACK))
        load_scales(2, nc.scalar)
        load_x(0)
        load_scales(3, nc.scalar)
        nc.sync.dma_start(offsets[:], offs)
        nc.scalar.dma_start(out=w4_codes[:].bitcast(I32), in_=w4_words[0].bitcast(I32))
        load_wgo(0)
        for a in range(1, len(x_raw)):
            load_x(a)
            load_wgo(a)

        nc.vector.memset(window[:], 0.0)

        def interleave(copy, raw, name, tag):
            grouped = keep.tile([P, raw.shape[2], PACK], BF16, name=name, tag=tag, align_bytes=64)
            copy(
                out=grouped[:].rearrange("p (c i) t -> p c t i", i=RUN),
                in_=raw.rearrange("p t (c i) -> p c t i", i=RUN),
            )
            return grouped

        def quantize(grouped, name):
            width = grouped.shape[1]
            codes = keep.tile([P, width], U32, name=name + "_codes", align_bytes=64)
            plane = keep.tile([P, width], U8, name=name + "_plane", align_bytes=64)
            nc.vector.quantize_mx(
                out=codes[:].bitcast(FP8X4), scales=plane[:], in_=grouped[:].rearrange("p j t -> p (j t)")
            )
            return codes, plane

        def raw_tokens(i):
            a, j0 = divmod(first_token[i], X_LOAD)
            return x_raw[a][:, :, j0 : j0 + CHUNKS[i]]

        def round_chunk(i):
            if i < VECTOR_CHUNKS:
                return interleave(nc.vector.tensor_copy, raw_tokens(i), "x_bf%d" % i, "x_bf_vector")
            return interleave(nc.scalar.copy, raw_tokens(i), "x_bf%d" % i, "x_bf%d" % i)

        def product(name, bank, w_codes, w_plane, x_mx):
            codes, plane = x_mx
            acc = psum.tile([M, codes.shape[1]], F32, name=name, tag="bank%d" % bank)
            nc.tensor.matmul_mx(
                out=acc[:], lhsT=w_codes, lhsT_scale=w_plane[:],
                rhs=codes[:].bitcast(FP8X4), rhs_scale=plane[:], start=True, stop=True,
            )
            return acc

        def gate_sum(i, x_mx):
            return product("e%d" % i, i + 1, w4_codes[:].bitcast(FP4X4), w4_plane, x_mx)

        def up_sum(i, x_mx):
            return product("u%d" % i, i, w8_codes[:].bitcast(FP8X4), w8_plane, x_mx)

        def place(i, e, u):
            n = CHUNKS[i]
            if VECTOR_CHUNKS <= i + 1 <= last:
                gate = raw_tokens(i + 1)[:, 0, 0:n]
            else:
                gate_tile = keep.tile([M, n], F32, name="gate%d" % i)
                gate = gate_tile[:]
            nc.scalar.activation(out=gate, in_=e[:], func=SILU)

            a = max(b for b, j in enumerate(wgo_first) if j <= first_token[i])
            j0 = first_token[i] - wgo_first[a]
            up = keep.tile([M, n], F32, name="up%d" % i)
            nc.vector.tensor_tensor(up[:], u[:], wgo_sb[a][:, j0 : j0 + n], MULT)

            entries = slice(first_token[i] // LIST_ROWS, (first_token[i] + n) // LIST_ROWS)
            nc.vector.tensor_tensor(window[:].indirect(offsets[:, entries]), gate, up[:], MULT)

        w8_codes, w8_plane = quantize(interleave(nc.vector.tensor_copy, w8_raw[:], "w8_bf", "w8_bf"), "w8")
        x_mx = quantize(round_chunk(0), "x0")
        e = gate_sum(0, x_mx)
        u = up_sum(0, x_mx)
        grouped_next = round_chunk(1)
        for i in range(last):
            x_mx = quantize(grouped_next, "x%d" % (i + 1))
            e_next = gate_sum(i + 1, x_mx)
            place(i, e, u)
            e, u = e_next, up_sum(i + 1, x_mx)
            if i + 2 <= last:
                grouped_next = round_chunk(i + 2)
        place(last, e, u)

        nc.sync.dma_start(out=out, in_=window[:])
